import numpy as np
import ml_dtypes


def mxq(x, axis, fmt="e4m3"):
    dtype, down = {"e4m3": (ml_dtypes.float8_e4m3fn, 7), "e5m2": (ml_dtypes.float8_e5m2, 14)}[fmt]
    v = np.moveaxis(np.asarray(x, np.float32).astype(ml_dtypes.bfloat16).astype(np.float64), axis, -1)
    blocks = v.reshape(v.shape[:-1] + (-1, 32))
    amax = np.abs(blocks).max(-1, keepdims=True)
    byte = np.maximum(np.where(amax > 0, np.frexp(amax)[1] - 1 + 127, 0) - down, 1)
    scale = np.exp2(byte - 127.0)
    codes = (blocks / scale).astype(np.float32).astype(dtype).astype(np.float64)
    return np.moveaxis((codes * scale).reshape(v.shape), -1, axis)


WIDE = False


def mx_kscale(k):
    if not WIDE:
        return np.ones(k)
    levels = np.array([10, -10, 5, -5, 0])
    if k % 512:
        return np.exp2(np.random.permutation(np.resize(levels, k // 32))).repeat(32)
    a = np.empty((k // 512, 16))
    for p in range(k // 512):
        a[p, :8] = np.random.permutation(np.resize(levels, 8))
        for g in range(8):
            far = levels[np.abs(levels - a[p, g]) >= 10]
            a[p, g + 8] = far[np.random.randint(len(far))]
    return np.exp2(a.ravel()).repeat(32)


def f64(x):
    return np.asarray(x).astype(np.float64)


def striped(idx):
    return np.tile(idx.reshape(-1, 16).T, (8, 1)).astype(np.uint16)


def unstriped(offs):
    return offs[:16].T.reshape(-1).astype(np.int64)


def pack_weight(w):
    k, n = w.shape
    w = f64(np.asarray(w, np.float32).astype(ml_dtypes.bfloat16)).reshape(k // 32, 32, n)
    amax = np.abs(w).max(1)
    byte = np.clip(np.where(amax > 0, np.frexp(amax)[1] - 1 + 127 - 7, 1), 1, 254)
    scaled = (w * np.exp2(127.0 - byte)[:, None, :]).reshape(k, n).astype(np.float32)
    words = np.ascontiguousarray(scaled.reshape(k // 512, 128, 4, n).transpose(0, 1, 3, 2)).astype(ml_dtypes.float8_e4m3fn).view(np.uint8)
    return words, np.ascontiguousarray(byte.astype(np.uint8).reshape(k // 512, 16, n))


def unpack_weight(words, scales):
    g, p, n, _ = words.shape
    vals = np.ascontiguousarray(words).view(ml_dtypes.float8_e4m3fn).astype(np.float64) * np.repeat(np.exp2(scales.astype(np.float64) - 127.0), 8, axis=1)[..., None]
    return vals.transpose(0, 1, 3, 2).reshape(g * 512, n)


K, T, E, C, N = 512, 4096, 8, 256, 256


def by_expert(wq, xq):
    return np.concatenate([wq[e].T @ xq[:, e * C:(e + 1) * C] for e in range(E)], axis=1)


def setup_inputs():
    n = np.random.standard_normal
    s = mx_kscale(K)[:, None]
    packed = [pack_weight(m) for m in n((E, K, N)) / np.sqrt(K) / s[None]]
    return {
        "xT": (n((K, T)) * s).astype(np.float32),
        "w_words": np.stack([m[0] for m in packed]),
        "w_scales": np.stack([m[1] for m in packed]),
        "gate": np.tile(np.random.uniform(0.2, 1.0, E * C), (N, 1)).astype(np.float32),
        "offs": striped(np.random.permutation(T)[:E * C]),
    }


def reference(xT, w_words, w_scales, gate, offs):
    idx = unstriped(offs)
    xq = mxq(f64(xT)[:, idx], 0, "e4m3")
    w = np.stack([unpack_weight(w_words[e], w_scales[e]) for e in range(E)])
    y = by_expert(w, xq)
    out = np.zeros((N, T))
    out[:, idx] = f64(gate) * y
    return out

@@ -1,0 +1,122 @@
+from contextlib import ExitStack
+
+import concourse.mybir as mybir
+
+K, T, E, C, N = 512, 4096, 8, 256, 256
+FLOPS = 2 * K * N * E * C
+
+F32 = mybir.dt.float32
+BF16 = mybir.dt.bfloat16
+I32 = mybir.dt.int32
+U32 = mybir.dt.uint32
+U16 = mybir.dt.uint16
+U8 = mybir.dt.uint8
+FP8X4 = mybir.dt.float8_e4m3fn_x4
+MULT = mybir.AluOpType.mult
+
+P = 128
+PACK = 4
+SLOTS = E * C
+BLOCKS = N // P
+HALF = 1024
+SLICE = 512
+PER = 16
+
+SCATTERS = ((0, 0, 512), (1, 0, 512), (0, 512, 512), (0, 1024, 1024), (1, 512, 1536))
+
+
+def tile_routed_moe_kernel(tc, xT, w_words, w_scales, gate, offs, out):
+    nc = tc.nc
+    with ExitStack() as ctx:
+        lists = ctx.enter_context(tc.tile_pool(name="lists", bufs=1))
+        keep = ctx.enter_context(tc.tile_pool(name="keep", bufs=1))
+        psum = ctx.enter_context(tc.psum_pool(name="psum", bufs=1))
+
+        offsets = lists.tile([P, SLOTS // PER], U16, name="offsets")
+        nc.sync.dma_start(offsets[:], offs)
+
+        def listed(first, count):
+            return offsets[:, first // PER : (first + count) // PER]
+
+        x_view = xT.rearrange("(p t) n -> p t n", t=PACK)
+        planes = []
+        for t in range(PACK):
+            plane = keep.tile([P, T], F32, name="plane%d" % t)
+            nc.sync.dma_start(out=plane[:], in_=x_view[:, t, :])
+            planes.append(plane)
+
+        w_scale = keep.tile([P, E * N], U8, name="w_scale", align_bytes=64)
+        nc.vector.memset(w_scale[:].bitcast(I32), 0)
+        windows = []
+        for b in range(BLOCKS):
+            window = keep.tile([P, T], F32, name="window%d" % b)
+            nc.vector.memset(window[:], 0.0)
+            windows.append(window)
+
+        ws_view = w_scales.bitcast(I32).rearrange("e a (q r) n -> r q (e a) n", r=4)
+        for r in range(4):
+            nc.sync.dma_start(
+                out=w_scale[r:P:32, :].bitcast(I32).rearrange("q (e n) -> q e n", e=E),
+                in_=ws_view[r],
+            )
+        w_view = w_words.rearrange("e a p n r -> p (e a) (n r)").bitcast(I32)
+        w_codes = []
+        for s in range(SLOTS // SLICE):
+            wc = keep.tile([P, 2, N], I32, name="w_codes%d" % s, align_bytes=64)
+            nc.sync.dma_start(out=wc[:], in_=w_view[:, 2 * s : 2 * s + 2, :])
+            w_codes.append(wc)
+        gates = []
+        for b in range(BLOCKS):
+            g = keep.tile([P, SLOTS], F32, name="gate%d" % b)
+            nc.sync.dma_start(out=g[:], in_=gate[b * P : (b + 1) * P, :])
+            gates.append(g)
+
+        gathered = [keep.tile([P, PACK, HALF], F32, name="gathered%d" % h) for h in range(SLOTS // HALF)]
+        for t in range(PACK - 1):
+            for h in range(SLOTS // HALF):
+                nc.vector.tensor_copy(out=gathered[h][:, t, :], in_=planes[t][:].indirect(listed(h * HALF, HALF)))
+        for s in range(SLOTS // SLICE):
+            h, c0 = divmod(s * SLICE, HALF)
+            nc.vector.tensor_copy(
+                out=gathered[h][:, PACK - 1, c0 : c0 + SLICE],
+                in_=planes[PACK - 1][:].indirect(listed(s * SLICE, SLICE)),
+            )
+
+        sums = [keep.tile([P, SLOTS], F32, name="sums%d" % b) for b in range(BLOCKS)]
+        for s in range(SLOTS // SLICE):
+            h, c0 = divmod(s * SLICE, HALF)
+            grouped = keep.tile([P, SLICE, PACK], BF16, name="grouped%d" % s, align_bytes=64)
+            nc.scalar.copy(out=grouped[:], in_=gathered[h][:, :, c0 : c0 + SLICE].rearrange("p t n -> p n t"))
+            codes = keep.tile([P, SLICE], U32, name="codes%d" % s, align_bytes=64)
+            scales = keep.tile([P, SLICE], U8, name="scales%d" % s, align_bytes=64)
+            nc.vector.quantize_mx(
+                out=codes[:].bitcast(FP8X4),
+                scales=scales[:],
+                in_=grouped[:].rearrange("p n t -> p (n t)"),
+            )
+            for b in range(BLOCKS):
+                acc = psum.tile([P, SLICE], F32, name="acc%d_%d" % (b, s))
+                for j in range(SLICE // C):
+                    e = s * (SLICE // C) + j
+                    nc.tensor.matmul_mx(
+                        out=acc[:, j * C : (j + 1) * C],
+                        lhsT=w_codes[s][:, j, b * P : (b + 1) * P].bitcast(FP8X4),
+                        lhsT_scale=w_scale[:, e * N + b * P : e * N + (b + 1) * P],
+                        rhs=codes[:, j * C : (j + 1) * C].bitcast(FP8X4),
+                        rhs_scale=scales[:, j * C : (j + 1) * C],
+                        start=True,
+                        stop=True,
+                    )
+                nc.scalar.copy(out=sums[b][:, s * SLICE : (s + 1) * SLICE], in_=acc[:])
+
+        left = [sum(n for (bb, f, n) in SCATTERS if bb == b) for b in range(BLOCKS)]
+        for b, first, count in SCATTERS:
+            nc.vector.tensor_tensor(
+                out=windows[b][:].indirect(listed(first, count)),
+                in0=sums[b][:, first : first + count],
+                in1=gates[b][:, first : first + count],
+                op=MULT,
+            )
+            left[b] -= count
+            if left[b] == 0:
+                nc.sync.dma_start(out=out[b * P : (b + 1) * P, :], in_=windows[b][:])

@@ -22,8 +22,6 @@ HALF = 1024
 SLICE = 512
 PER = 16
 
-SCATTERS = ((0, 0, 512), (1, 0, 512), (0, 512, 512), (0, 1024, 1024), (1, 512, 1536))
-
 
 def tile_routed_moe_kernel(tc, xT, w_words, w_scales, gate, offs, out):
     nc = tc.nc
@@ -39,32 +37,28 @@ def tile_routed_moe_kernel(tc, xT, w_words, w_scales, gate, offs, out):
             return offsets[:, first // PER : (first + count) // PER]
 
         x_view = xT.rearrange("(p t) n -> p t n", t=PACK)
+        w_scale = keep.tile([P, E * N], U8, name="w_scale", align_bytes=64)
+        nc.vector.memset(w_scale[:].bitcast(I32), 0)
+        ws_view = w_scales.bitcast(I32).rearrange("e a (q r) n -> r q (e a) n", r=4)
         planes = []
         for t in range(PACK):
+            if t == PACK - 1:
+                for r in range(4):
+                    nc.sync.dma_start(
+                        out=w_scale[r:P:32, :].bitcast(I32).rearrange("q (e n) -> q e n", e=E),
+                        in_=ws_view[r],
+                    )
             plane = keep.tile([P, T], F32, name="plane%d" % t)
             nc.sync.dma_start(out=plane[:], in_=x_view[:, t, :])
             planes.append(plane)
 
-        w_scale = keep.tile([P, E * N], U8, name="w_scale", align_bytes=64)
-        nc.vector.memset(w_scale[:].bitcast(I32), 0)
-        windows = []
-        for b in range(BLOCKS):
-            window = keep.tile([P, T], F32, name="window%d" % b)
-            nc.vector.memset(window[:], 0.0)
-            windows.append(window)
+        windows = [keep.tile([P, T], F32, name="window%d" % b) for b in range(BLOCKS)]
+        nc.vector.memset(windows[0][:], 0.0)
+        nc.gpsimd.memset(windows[1][:], 0.0)
 
-        ws_view = w_scales.bitcast(I32).rearrange("e a (q r) n -> r q (e a) n", r=4)
-        for r in range(4):
-            nc.sync.dma_start(
-                out=w_scale[r:P:32, :].bitcast(I32).rearrange("q (e n) -> q e n", e=E),
-                in_=ws_view[r],
-            )
         w_view = w_words.rearrange("e a p n r -> p (e a) (n r)").bitcast(I32)
-        w_codes = []
-        for s in range(SLOTS // SLICE):
-            wc = keep.tile([P, 2, N], I32, name="w_codes%d" % s, align_bytes=64)
-            nc.sync.dma_start(out=wc[:], in_=w_view[:, 2 * s : 2 * s + 2, :])
-            w_codes.append(wc)
+        w_codes = keep.tile([P, E, N], I32, name="w_codes", align_bytes=64)
+        nc.sync.dma_start(out=w_codes[:], in_=w_view)
         gates = []
         for b in range(BLOCKS):
             g = keep.tile([P, SLOTS], F32, name="gate%d" % b)
@@ -72,51 +66,76 @@ def tile_routed_moe_kernel(tc, xT, w_words, w_scales, gate, offs, out):
             gates.append(g)
 
         gathered = [keep.tile([P, PACK, HALF], F32, name="gathered%d" % h) for h in range(SLOTS // HALF)]
-        for t in range(PACK - 1):
-            for h in range(SLOTS // HALF):
-                nc.vector.tensor_copy(out=gathered[h][:, t, :], in_=planes[t][:].indirect(listed(h * HALF, HALF)))
-        for s in range(SLOTS // SLICE):
-            h, c0 = divmod(s * SLICE, HALF)
+        sums = [keep.tile([P, SLOTS], F32, name="sums%d" % b) for b in range(BLOCKS)]
+        grouped = [keep.tile([P, SLICE, PACK], BF16, name="grouped%d" % s, align_bytes=64) for s in range(SLOTS // SLICE)]
+        codes = [keep.tile([P, SLICE], U32, name="codes%d" % s, align_bytes=64) for s in range(SLOTS // SLICE)]
+        scales = [keep.tile([P, SLICE], U8, name="scales%d" % s, align_bytes=64) for s in range(SLOTS // SLICE)]
+
+        def gather(t, first, count):
+            h, c0 = divmod(first, HALF)
             nc.vector.tensor_copy(
-                out=gathered[h][:, PACK - 1, c0 : c0 + SLICE],
-                in_=planes[PACK - 1][:].indirect(listed(s * SLICE, SLICE)),
+                out=gathered[h][:, t, c0 : c0 + count],
+                in_=planes[t][:].indirect(listed(first, count)),
             )
 
-        sums = [keep.tile([P, SLOTS], F32, name="sums%d" % b) for b in range(BLOCKS)]
-        for s in range(SLOTS // SLICE):
+        def interleave(copy, s, t0):
             h, c0 = divmod(s * SLICE, HALF)
-            grouped = keep.tile([P, SLICE, PACK], BF16, name="grouped%d" % s, align_bytes=64)
-            nc.scalar.copy(out=grouped[:], in_=gathered[h][:, :, c0 : c0 + SLICE].rearrange("p t n -> p n t"))
-            codes = keep.tile([P, SLICE], U32, name="codes%d" % s, align_bytes=64)
-            scales = keep.tile([P, SLICE], U8, name="scales%d" % s, align_bytes=64)
-            nc.vector.quantize_mx(
-                out=codes[:].bitcast(FP8X4),
-                scales=scales[:],
-                in_=grouped[:].rearrange("p n t -> p (n t)"),
+            copy(
+                out=grouped[s][:, :, t0 : t0 + 2],
+                in_=gathered[h][:, t0 : t0 + 2, c0 : c0 + SLICE].rearrange("p t n -> p n t"),
             )
+
+        def quantize(s):
+            nc.vector.quantize_mx(
+                out=codes[s][:].bitcast(FP8X4),
+                scales=scales[s][:],
+                in_=grouped[s][:].rearrange("p n t -> p (n t)"),
+            )
+
+        def multiply(s):
             for b in range(BLOCKS):
                 acc = psum.tile([P, SLICE], F32, name="acc%d_%d" % (b, s))
                 for j in range(SLICE // C):
                     e = s * (SLICE // C) + j
                     nc.tensor.matmul_mx(
                         out=acc[:, j * C : (j + 1) * C],
-                        lhsT=w_codes[s][:, j, b * P : (b + 1) * P].bitcast(FP8X4),
+                        lhsT=w_codes[:, e, b * P : (b + 1) * P].bitcast(FP8X4),
                         lhsT_scale=w_scale[:, e * N + b * P : e * N + (b + 1) * P],
-                        rhs=codes[:, j * C : (j + 1) * C].bitcast(FP8X4),
-                        rhs_scale=scales[:, j * C : (j + 1) * C],
+                        rhs=codes[s][:, j * C : (j + 1) * C].bitcast(FP8X4),
+                        rhs_scale=scales[s][:, j * C : (j + 1) * C],
                         start=True,
                         stop=True,
                     )
                 nc.scalar.copy(out=sums[b][:, s * SLICE : (s + 1) * SLICE], in_=acc[:])
 
-        left = [sum(n for (bb, f, n) in SCATTERS if bb == b) for b in range(BLOCKS)]
-        for b, first, count in SCATTERS:
+        def scatter(b, first, count):
             nc.vector.tensor_tensor(
                 out=windows[b][:].indirect(listed(first, count)),
                 in0=sums[b][:, first : first + count],
                 in1=gates[b][:, first : first + count],
                 op=MULT,
             )
-            left[b] -= count
-            if left[b] == 0:
-                nc.sync.dma_start(out=out[b * P : (b + 1) * P, :], in_=windows[b][:])
+
+        for t in range(2):
+            gather(t, 0, HALF)
+            gather(t, HALF, HALF)
+        for s in range(4):
+            interleave(nc.scalar.copy, s, 0)
+        gather(2, 0, HALF)
+        gather(2, HALF, HALF)
+        gather(3, 0, SLICE)
+        interleave(nc.vector.tensor_copy, 0, 2)
+        quantize(0)
+        multiply(0)
+        for s in range(1, 4):
+            gather(3, s * SLICE, SLICE)
+            interleave(nc.scalar.copy, s, 2)
+        for s in range(1, 4):
+            quantize(s)
+            multiply(s)
+        scatter(0, 0, SLICE)
+        scatter(1, 0, SLICE)
+        scatter(0, SLICE, 3 * SLICE)
+        nc.sync.dma_start(out=out[0:P, :], in_=windows[0][:])
+        scatter(1, SLICE, 3 * SLICE)
+        nc.sync.dma_start(out=out[P : 2 * P, :], in_=windows[1][:])

@@ -92,7 +92,7 @@ def tile_routed_moe_kernel(tc, xT, w_words, w_scales, gate, offs, out):
                 in_=grouped[s][:].rearrange("p n t -> p (n t)"),
             )
 
-        def multiply(s):
+        def multiply(s, copies):
             for b in range(BLOCKS):
                 acc = psum.tile([P, SLICE], F32, name="acc%d_%d" % (b, s))
                 for j in range(SLICE // C):
@@ -106,7 +106,7 @@ def tile_routed_moe_kernel(tc, xT, w_words, w_scales, gate, offs, out):
                         start=True,
                         stop=True,
                     )
-                nc.scalar.copy(out=sums[b][:, s * SLICE : (s + 1) * SLICE], in_=acc[:])
+                copies[b](out=sums[b][:, s * SLICE : (s + 1) * SLICE], in_=acc[:])
 
         def scatter(b, first, count):
             nc.vector.tensor_tensor(
@@ -123,16 +123,17 @@ def tile_routed_moe_kernel(tc, xT, w_words, w_scales, gate, offs, out):
             interleave(nc.scalar.copy, s, 0)
         gather(2, 0, HALF)
         gather(2, HALF, HALF)
-        gather(3, 0, SLICE)
-        interleave(nc.vector.tensor_copy, 0, 2)
-        quantize(0)
-        multiply(0)
-        for s in range(1, 4):
+        for s in range(2):
             gather(3, s * SLICE, SLICE)
+            interleave(nc.scalar.copy, s, 2)
+        gather(3, HALF, HALF)
+        quantize(0)
+        multiply(0, (nc.vector.tensor_copy, nc.scalar.copy))
+        for s in range(2, 4):
             interleave(nc.scalar.copy, s, 2)
         for s in range(1, 4):
             quantize(s)
-            multiply(s)
+            multiply(s, (nc.scalar.copy, nc.scalar.copy))
         scatter(0, 0, SLICE)
         scatter(1, 0, SLICE)
         scatter(0, SLICE, 3 * SLICE)

@@ -54,7 +54,7 @@ def tile_routed_moe_kernel(tc, xT, w_words, w_scales, gate, offs, out):
 
         windows = [keep.tile([P, T], F32, name="window%d" % b) for b in range(BLOCKS)]
         nc.vector.memset(windows[0][:], 0.0)
-        nc.gpsimd.memset(windows[1][:], 0.0)
+        nc.vector.memset(windows[1][:], 0.0)
 
         w_view = w_words.rearrange("e a p n r -> p (e a) (n r)").bitcast(I32)
         w_codes = keep.tile([P, E, N], I32, name="w_codes", align_bytes=64)

@@ -54,7 +54,7 @@ def tile_routed_moe_kernel(tc, xT, w_words, w_scales, gate, offs, out):
 
         windows = [keep.tile([P, T], F32, name="window%d" % b) for b in range(BLOCKS)]
         nc.vector.memset(windows[0][:], 0.0)
-        nc.vector.memset(windows[1][:], 0.0)
+        nc.gpsimd.memset(windows[1][:], 0.0)
 
         w_view = w_words.rearrange("e a p n r -> p (e a) (n r)").bitcast(I32)
         w_codes = keep.tile([P, E, N], I32, name="w_codes", align_bytes=64)
@@ -123,18 +123,19 @@ def tile_routed_moe_kernel(tc, xT, w_words, w_scales, gate, offs, out):
             interleave(nc.scalar.copy, s, 0)
         gather(2, 0, HALF)
         gather(2, HALF, HALF)
-        for s in range(2):
+        for s in range(3):
             gather(3, s * SLICE, SLICE)
             interleave(nc.scalar.copy, s, 2)
-        gather(3, HALF, HALF)
         quantize(0)
-        multiply(0, (nc.vector.tensor_copy, nc.scalar.copy))
-        for s in range(2, 4):
-            interleave(nc.scalar.copy, s, 2)
-        for s in range(1, 4):
+        multiply(0, (nc.scalar.copy, nc.scalar.copy))
+        gather(3, 3 * SLICE, SLICE)
+        interleave(nc.scalar.copy, 3, 2)
+        for s in range(1, 3):
             quantize(s)
             multiply(s, (nc.scalar.copy, nc.scalar.copy))
         scatter(0, 0, SLICE)
+        quantize(3)
+        multiply(3, (nc.scalar.copy, nc.scalar.copy))
         scatter(1, 0, SLICE)
         scatter(0, SLICE, 3 * SLICE)
         nc.sync.dma_start(out=out[0:P, :], in_=windows[0][:])

@@ -54,7 +54,7 @@ def tile_routed_moe_kernel(tc, xT, w_words, w_scales, gate, offs, out):
 
         windows = [keep.tile([P, T], F32, name="window%d" % b) for b in range(BLOCKS)]
         nc.vector.memset(windows[0][:], 0.0)
-        nc.gpsimd.memset(windows[1][:], 0.0)
+        nc.vector.memset(windows[1][:], 0.0)
 
         w_view = w_words.rearrange("e a p n r -> p (e a) (n r)").bitcast(I32)
         w_codes = keep.tile([P, E, N], I32, name="w_codes", align_bytes=64)
@@ -65,24 +65,22 @@ def tile_routed_moe_kernel(tc, xT, w_words, w_scales, gate, offs, out):
             nc.sync.dma_start(out=g[:], in_=gate[b * P : (b + 1) * P, :])
             gates.append(g)
 
-        gathered = [keep.tile([P, PACK, HALF], F32, name="gathered%d" % h) for h in range(SLOTS // HALF)]
+        gathered = keep.tile([P, PACK, SLOTS], F32, name="gathered")
         sums = [keep.tile([P, SLOTS], F32, name="sums%d" % b) for b in range(BLOCKS)]
         grouped = [keep.tile([P, SLICE, PACK], BF16, name="grouped%d" % s, align_bytes=64) for s in range(SLOTS // SLICE)]
         codes = [keep.tile([P, SLICE], U32, name="codes%d" % s, align_bytes=64) for s in range(SLOTS // SLICE)]
         scales = [keep.tile([P, SLICE], U8, name="scales%d" % s, align_bytes=64) for s in range(SLOTS // SLICE)]
 
         def gather(t, first, count):
-            h, c0 = divmod(first, HALF)
             nc.vector.tensor_copy(
-                out=gathered[h][:, t, c0 : c0 + count],
+                out=gathered[:, t, first : first + count],
                 in_=planes[t][:].indirect(listed(first, count)),
             )
 
         def interleave(copy, s, t0):
-            h, c0 = divmod(s * SLICE, HALF)
             copy(
                 out=grouped[s][:, :, t0 : t0 + 2],
-                in_=gathered[h][:, t0 : t0 + 2, c0 : c0 + SLICE].rearrange("p t n -> p n t"),
+                in_=gathered[:, t0 : t0 + 2, s * SLICE : (s + 1) * SLICE].rearrange("p t n -> p n t"),
             )
 
         def quantize(s):
@@ -116,13 +114,12 @@ def tile_routed_moe_kernel(tc, xT, w_words, w_scales, gate, offs, out):
                 op=MULT,
             )
 
-        for t in range(2):
-            gather(t, 0, HALF)
-            gather(t, HALF, HALF)
+        gather(0, 0, SLOTS)
+        gather(1, 0, HALF)
+        gather(1, HALF, HALF)
         for s in range(4):
             interleave(nc.scalar.copy, s, 0)
-        gather(2, 0, HALF)
-        gather(2, HALF, HALF)
+        gather(2, 0, SLOTS)
         for s in range(3):
             gather(3, s * SLICE, SLICE)
             interleave(nc.scalar.copy, s, 2)

@@ -31,7 +31,6 @@ def tile_routed_moe_kernel(tc, xT, w_words, w_scales, gate, offs, out):
         psum = ctx.enter_context(tc.psum_pool(name="psum", bufs=1))
 
         offsets = lists.tile([P, SLOTS // PER], U16, name="offsets")
-        nc.sync.dma_start(offsets[:], offs)
 
         def listed(first, count):
             return offsets[:, first // PER : (first + count) // PER]
@@ -51,6 +50,8 @@ def tile_routed_moe_kernel(tc, xT, w_words, w_scales, gate, offs, out):
             plane = keep.tile([P, T], F32, name="plane%d" % t)
             nc.sync.dma_start(out=plane[:], in_=x_view[:, t, :])
             planes.append(plane)
+            if t == 0:
+                nc.sync.dma_start(offsets[:], offs)
 
         windows = [keep.tile([P, T], F32, name="window%d" % b) for b in range(BLOCKS)]
         nc.vector.memset(windows[0][:], 0.0)

from contextlib import ExitStack

import concourse.mybir as mybir

K, T, E, C, N = 512, 4096, 8, 256, 256
FLOPS = 2 * K * N * E * C

F32 = mybir.dt.float32
BF16 = mybir.dt.bfloat16
I32 = mybir.dt.int32
U32 = mybir.dt.uint32
U16 = mybir.dt.uint16
U8 = mybir.dt.uint8
FP8X4 = mybir.dt.float8_e4m3fn_x4
MULT = mybir.AluOpType.mult

P = 128
PACK = 4
SLOTS = E * C
BLOCKS = N // P
HALF = 1024
SLICE = 512
PER = 16


def tile_routed_moe_kernel(tc, xT, w_words, w_scales, gate, offs, out):
    nc = tc.nc
    with ExitStack() as ctx:
        lists = ctx.enter_context(tc.tile_pool(name="lists", bufs=1))
        keep = ctx.enter_context(tc.tile_pool(name="keep", bufs=1))
        psum = ctx.enter_context(tc.psum_pool(name="psum", bufs=1))

        offsets = lists.tile([P, SLOTS // PER], U16, name="offsets")

        def listed(first, count):
            return offsets[:, first // PER : (first + count) // PER]

        x_view = xT.rearrange("(p t) n -> p t n", t=PACK)
        w_scale = keep.tile([P, E * N], U8, name="w_scale", align_bytes=64)
        nc.vector.memset(w_scale[:].bitcast(I32), 0)
        ws_view = w_scales.bitcast(I32).rearrange("e a (q r) n -> r q (e a) n", r=4)
        planes = []
        for t in range(PACK):
            if t == PACK - 1:
                for r in range(4):
                    nc.sync.dma_start(
                        out=w_scale[r:P:32, :].bitcast(I32).rearrange("q (e n) -> q e n", e=E),
                        in_=ws_view[r],
                    )
            plane = keep.tile([P, T], F32, name="plane%d" % t)
            nc.sync.dma_start(out=plane[:], in_=x_view[:, t, :])
            planes.append(plane)
            if t == 0:
                nc.sync.dma_start(offsets[:], offs)

        windows = [keep.tile([P, T], F32, name="window%d" % b) for b in range(BLOCKS)]
        nc.vector.memset(windows[0][:], 0.0)
        nc.vector.memset(windows[1][:], 0.0)

        w_view = w_words.rearrange("e a p n r -> p (e a) (n r)").bitcast(I32)
        w_codes = keep.tile([P, E, N], I32, name="w_codes", align_bytes=64)
        nc.sync.dma_start(out=w_codes[:], in_=w_view)
        gates = []
        for b in range(BLOCKS):
            g = keep.tile([P, SLOTS], F32, name="gate%d" % b)
            nc.sync.dma_start(out=g[:], in_=gate[b * P : (b + 1) * P, :])
            gates.append(g)

        gathered = keep.tile([P, PACK, SLOTS], F32, name="gathered")
        sums = [keep.tile([P, SLOTS], F32, name="sums%d" % b) for b in range(BLOCKS)]
        grouped = [keep.tile([P, SLICE, PACK], BF16, name="grouped%d" % s, align_bytes=64) for s in range(SLOTS // SLICE)]
        codes = [keep.tile([P, SLICE], U32, name="codes%d" % s, align_bytes=64) for s in range(SLOTS // SLICE)]
        scales = [keep.tile([P, SLICE], U8, name="scales%d" % s, align_bytes=64) for s in range(SLOTS // SLICE)]

        def gather(t, first, count):
            nc.vector.tensor_copy(
                out=gathered[:, t, first : first + count],
                in_=planes[t][:].indirect(listed(first, count)),
            )

        def interleave(copy, s, t0):
            copy(
                out=grouped[s][:, :, t0 : t0 + 2],
                in_=gathered[:, t0 : t0 + 2, s * SLICE : (s + 1) * SLICE].rearrange("p t n -> p n t"),
            )

        def quantize(s):
            nc.vector.quantize_mx(
                out=codes[s][:].bitcast(FP8X4),
                scales=scales[s][:],
                in_=grouped[s][:].rearrange("p n t -> p (n t)"),
            )

        def multiply(s, copies):
            for b in range(BLOCKS):
                acc = psum.tile([P, SLICE], F32, name="acc%d_%d" % (b, s))
                for j in range(SLICE // C):
                    e = s * (SLICE // C) + j
                    nc.tensor.matmul_mx(
                        out=acc[:, j * C : (j + 1) * C],
                        lhsT=w_codes[:, e, b * P : (b + 1) * P].bitcast(FP8X4),
                        lhsT_scale=w_scale[:, e * N + b * P : e * N + (b + 1) * P],
                        rhs=codes[s][:, j * C : (j + 1) * C].bitcast(FP8X4),
                        rhs_scale=scales[s][:, j * C : (j + 1) * C],
                        start=True,
                        stop=True,
                    )
                copies[b](out=sums[b][:, s * SLICE : (s + 1) * SLICE], in_=acc[:])

        def scatter(b, first, count):
            nc.vector.tensor_tensor(
                out=windows[b][:].indirect(listed(first, count)),
                in0=sums[b][:, first : first + count],
                in1=gates[b][:, first : first + count],
                op=MULT,
            )

        gather(0, 0, SLOTS)
        gather(1, 0, HALF)
        gather(1, HALF, HALF)
        for s in range(4):
            interleave(nc.scalar.copy, s, 0)
        gather(2, 0, SLOTS)
        for s in range(3):
            gather(3, s * SLICE, SLICE)
            interleave(nc.scalar.copy, s, 2)
        quantize(0)
        multiply(0, (nc.scalar.copy, nc.scalar.copy))
        gather(3, 3 * SLICE, SLICE)
        interleave(nc.scalar.copy, 3, 2)
        for s in range(1, 3):
            quantize(s)
            multiply(s, (nc.scalar.copy, nc.scalar.copy))
        scatter(0, 0, SLICE)
        quantize(3)
        multiply(3, (nc.scalar.copy, nc.scalar.copy))
        scatter(1, 0, SLICE)
        scatter(0, SLICE, 3 * SLICE)
        nc.sync.dma_start(out=out[0:P, :], in_=windows[0][:])
        scatter(1, SLICE, 3 * SLICE)
        nc.sync.dma_start(out=out[P : 2 * P, :], in_=windows[1][:])
